import numpy as np
CORES = [0,1,2,3,4,5,6,7]
N = 8
ROWS, COLS = 2, 4
def setup_inputs(rng):
    return {"x": rng.standard_normal((N, 128, 4), dtype=np.float32)}
def reference(x):
    g = x.astype(np.float64).reshape(ROWS, COLS, 128, 4)
    rs = g.sum(axis=1)
    cs = g.sum(axis=0)
    y1 = np.stack([rs[r // COLS] for r in range(N)]).astype(x.dtype)
    y2 = np.stack([cs[r % COLS] for r in range(N)]).astype(x.dtype)
    return {"y1": y1, "y2": y2}

from concourse.bass import DstId, RemoteDMATransfer
from concourse.mybir import AluOpType

ROWS, COLS = 2, 4

SCRATCH = {
    "own": ("dram", [128, 4], "float32"),
    "land": ("dram", [4, 128, 4], "float32"),
}
SEMAPHORES = ["loaded", "seeded", "arrived", "tree", "col"]


def rank_program(g, core, T, topo):
    rank = T.rank_of(core)
    if rank is None:
        return
    row, colm = divmod(rank, COLS)

    g.sync.dma_start(T.own[:], T.x[:]).then_inc(T.sem.loaded, 16)
    g.scalar.dma_start(T.y1[:], T.x[:]).then_inc(T.sem.seeded, 16)
    g.sync.dma_start(T.y2[:], T.x[:]).then_inc(T.sem.seeded, 16)

    dests = []
    for d in range(1, COLS):
        peer_col = (colm - d) % COLS
        dests.append((row * COLS + peer_col, d - 1))
    dests.append(((1 - row) * COLS + colm, 3))

    transfers = []
    for i, (peer, slot) in enumerate(dests):
        rid, pid, _se = topo.addr(T.cores[peer])
        transfers.append(RemoteDMATransfer(
            dst_ids=[DstId(rid=rid, pnc=pid)],
            dma_engine_mask=0xF << (4 * i),
            remote_sem=T.sem.arrived,
            src=T.own[:],
            dst=T.land[slot],
        ))
    g.wait_ge(T.sem.loaded, 16)
    g.remote_dma_fused(transfers, local_sem=T.sem.arrived)

    g.wait_ge(T.sem.arrived, 32)
    g.wait_ge(T.sem.seeded, 32)
    g.dma_start(T.land[0], T.land[1], accum_op=AluOpType.add).then_inc(T.sem.tree, 16)
    g.dma_start(T.y1[:], T.land[2], accum_op=AluOpType.add).then_inc(T.sem.tree, 16)
    g.dma_start(T.y2[:], T.land[3], accum_op=AluOpType.add).then_inc(T.sem.col, 16)

    g.wait_ge(T.sem.tree, 32)
    g.dma_start(T.y1[:], T.land[0], accum_op=AluOpType.add).then_inc(T.sem.tree, 16)
    g.wait_ge(T.sem.tree, 48)
    g.wait_ge(T.sem.col, 16)
